import numpy as np
import ml_dtypes


def mxq(x, axis, fmt="e4m3"):
    dtype, down = {"e4m3": (ml_dtypes.float8_e4m3fn, 7), "e5m2": (ml_dtypes.float8_e5m2, 14)}[fmt]
    v = np.moveaxis(np.asarray(x, np.float32).astype(ml_dtypes.bfloat16).astype(np.float64), axis, -1)
    blocks = v.reshape(v.shape[:-1] + (-1, 32))
    amax = np.abs(blocks).max(-1, keepdims=True)
    byte = np.maximum(np.where(amax > 0, np.frexp(amax)[1] - 1 + 127, 0) - down, 1)
    scale = np.exp2(byte - 127.0)
    codes = (blocks / scale).astype(np.float32).astype(dtype).astype(np.float64)
    return np.moveaxis((codes * scale).reshape(v.shape), -1, axis)


WIDE = False


def mx_kscale(k):
    if not WIDE:
        return np.ones(k)
    levels = np.array([10, -10, 5, -5, 0])
    if k % 512:
        return np.exp2(np.random.permutation(np.resize(levels, k // 32))).repeat(32)
    a = np.empty((k // 512, 16))
    for p in range(k // 512):
        a[p, :8] = np.random.permutation(np.resize(levels, 8))
        for g in range(8):
            far = levels[np.abs(levels - a[p, g]) >= 10]
            a[p, g + 8] = far[np.random.randint(len(far))]
    return np.exp2(a.ravel()).repeat(32)


BF16 = ml_dtypes.bfloat16


def bf(x):
    return np.asarray(x, np.float32).astype(BF16)


def f64(x):
    return np.asarray(x).astype(np.float64)

def planes(Y):
    n, m = Y.shape
    b = f64(bf(Y)).reshape(n // 32, 32, m)
    amax = np.abs(b).max(1)
    byte = np.clip(np.where(amax > 0, np.frexp(amax)[1] - 1 + 127 - 7, 1), 1, 254)
    codes = (b * np.exp2(127.0 - byte)[:, None, :]).reshape(n, m).astype(np.float32).astype(ml_dtypes.float8_e4m3fn).view(np.uint8)
    words = codes.reshape(n // 512, 128, 4, m).transpose(0, 1, 3, 2)
    return np.ascontiguousarray(words), np.ascontiguousarray(byte.astype(np.uint8).reshape(n // 512, 16, m))


B, D, N = 2048, 512, 1024

BETA = 0.625


def sigmoid(v):
    return 1.0 / (1.0 + np.exp(-v))


def setup_inputs():
    s, t = mx_kscale(D), mx_kscale(N)
    u = np.random.uniform(0.0, 1.0, (B, N))
    return {
        "x": bf(np.random.standard_normal((B, D))),
        "a": bf((1.0 + 0.1 * np.random.standard_normal(D)) * s),
        "w": bf(np.random.standard_normal((D, N)) / np.sqrt(D) / s[:, None] / t[None, :]),
        "e": bf((1.0 + 0.1 * np.random.standard_normal(N)) * t),
        "b": bf(0.5 * np.random.standard_normal(N)),
        "y": bf(np.where(u > 0.8, u + 0.01, u - 0.01)),
    }


def candidate_scores(x, a, w, e, b):
    xa = x * a[None, :]
    return e[None, :] * (mxq(xa, 1, "e4m3") @ mxq(w, 0, "e4m3")) + b[None, :]


def gbce_score_gradient(v, positive, beta):
    p = sigmoid(v)
    return np.where(positive, -beta * (1.0 - p), p)


def core(x, a, w, e, b, y):
    x, a, w, e, b, y = f64(x), f64(a), f64(w), f64(e), f64(b), f64(y)
    v = candidate_scores(x, a, w, e, b)
    positive = y > 0.8
    g = gbce_score_gradient(v, positive, BETA)
    k = g * e[None, :]
    return a[None, :] * (mxq(k, 1, "e4m3") @ mxq(w, 1, "e4m3").T)


def reference(x, a, w, e, b, y):
    R_out = core(x, a, w, e, b, y)
    words, scales = planes(R_out.T)
    return R_out, words, scales

@@ -1,0 +1,454 @@
+from contextlib import ExitStack
+
+import concourse.mybir as mybir
+from concourse.masks import make_identity
+
+B, D, N = 2048, 512, 1024
+BETA = 0.625
+THRESHOLD = 0.8
+FLOPS = 4 * B * D * N
+
+P = 128
+F32 = mybir.dt.float32
+BF16 = mybir.dt.bfloat16
+I32 = mybir.dt.int32
+U32 = mybir.dt.uint32
+U8 = mybir.dt.uint8
+FP8X4 = mybir.dt.float8_e4m3fn_x4
+ALU = mybir.AluOpType
+AF = mybir.ActivationFunctionType
+
+CHUNKS = [(0, 256), (256, 512), (768, 512), (1280, 512), (1792, 256)]
+
+
+def tile_gbcecandidatelossusergradient_x1_kernel(tc, x, a, w, e, b, y, out_0, out_1, out_2):
+    nc = tc.nc
+    words_out = out_1.rearrange("g p m t -> (g p) (m t)").bitcast(I32)
+    scales_out = out_2.rearrange("g q m -> (g q) m").bitcast(I32)
+
+    with ExitStack() as ctx:
+        const = ctx.enter_context(tc.tile_pool(name="const", bufs=1))
+        xpool = ctx.enter_context(tc.tile_pool(name="xpool", bufs=2))
+        kpool = ctx.enter_context(tc.tile_pool(name="kpool", bufs=2))
+        opool = ctx.enter_context(tc.tile_pool(name="opool", bufs=2))
+        ps_s = ctx.enter_context(tc.psum_pool(name="ps_s", bufs=2))
+        ps_z = ctx.enter_context(tc.psum_pool(name="ps_z", bufs=3))
+        ps_t = ctx.enter_context(tc.psum_pool(name="ps_t", bufs=3))
+        ctx.enter_context(tc.manual_schedule())
+
+        x_sb = const.tile([P, B // P, D], BF16)
+        y_sb = const.tile([P, B // P, N], BF16)
+        w_sb = const.tile([P, 4, N], BF16)
+        a_bf = const.tile([P, 4], BF16)
+        e_bf = const.tile([P, 2, 4], BF16)
+        b_bf = const.tile([P, 2, 4], BF16)
+        nc.scalar.dma_start(out=a_bf[:], in_=a.rearrange("(p t) -> p t", t=4))
+        nc.scalar.dma_start(out=e_bf[:], in_=e.rearrange("(g p t) -> p g t", g=2, t=4))
+        nc.scalar.dma_start(out=b_bf[:], in_=b.rearrange("(g p t) -> p g t", g=2, t=4))
+
+        def load_x(c):
+            b0, width = CHUNKS[c]
+            nc.sync.dma_start(
+                out=x_sb[:, b0 // P : (b0 + width) // P, :],
+                in_=x[b0 : b0 + width, :].rearrange("(j p) d -> p j d", p=P),
+            )
+
+        def load_y(b0, width):
+            nc.sync.dma_start(
+                out=y_sb[:, b0 // P : (b0 + width) // P, :],
+                in_=y[b0 : b0 + width, :].rearrange("(j p) n -> p j n", p=P),
+            )
+
+        def load_w(g):
+            nc.sync.dma_start(
+                out=w_sb[:, :, 512 * g : 512 * g + 512],
+                in_=w[:, 512 * g : 512 * g + 512].rearrange("(p j) n -> p j n", j=4),
+            )
+
+        load_x(0)
+        load_w(0)
+        load_y(0, 256)
+        load_w(1)
+        load_x(1)
+        load_y(256, 256)
+        load_y(512, 256)
+        load_x(2)
+        load_y(768, 512)
+        load_x(3)
+        load_y(1280, 512)
+        load_x(4)
+        load_y(1792, 256)
+
+        ident = const.tile([P, P], F32)
+        make_identity(nc, ident[:])
+        warm = const.tile([P, 1], F32)
+        nc.vector.memset(warm[:], 0.0)
+        warm_out = const.tile([P, 1], F32)
+        nc.scalar.activation(out=warm_out[:], in_=warm[:], func=AF.Sigmoid)
+
+        a_32 = const.tile([P, 4], F32)
+        e_32 = const.tile([P, 2, 4], F32)
+        ne_32 = const.tile([P, 2, 4], F32)
+        b_32 = const.tile([P, 2, 4], F32)
+
+        def constants():
+            nc.vector.tensor_copy(out=e_32[:], in_=e_bf[:])
+            nc.vector.tensor_copy(out=b_32[:], in_=b_bf[:])
+            nc.vector.tensor_scalar(out=ne_32[:], in0=e_bf[:], scalar1=-1.0, scalar2=None, op0=ALU.mult)
+            nc.vector.tensor_copy(out=a_32[:], in_=a_bf[:])
+
+        w1_grp = [const.tile([P, 2048], BF16, name="w1_grp%d" % g, align_bytes=64) for g in range(2)]
+        w1_codes = [const.tile([P, 512], U32, name="w1_codes%d" % g, align_bytes=64) for g in range(2)]
+        w1_scales = [const.tile([P, 512], U8, name="w1_scales%d" % g, align_bytes=64) for g in range(2)]
+        w2_grp = [const.tile([P, 512, 4], BF16, name="w2_grp%d" % g, align_bytes=64) for g in range(2)]
+        w2_codes = [const.tile([P, 512], U32, name="w2_codes%d" % g, align_bytes=64) for g in range(2)]
+        w2_scales = [const.tile([P, 512], U8, name="w2_scales%d" % g, align_bytes=64) for g in range(2)]
+
+        def w1_interleave(copy, g, u):
+            dst = w1_grp[g][:, 1024 * u : 1024 * u + 1024].rearrange("p (t m j) -> p t m j", t=2, j=4)
+            src = w_sb[:, :, 512 * g : 512 * g + 512].rearrange("p j (m t) -> p t m j", t=4)
+            copy(out=dst, in_=src[:, 2 * u : 2 * u + 2, :, :])
+
+        def quantize(codes, scales, grouped):
+            nc.vector.quantize_mx(out=codes.bitcast(FP8X4), scales=scales, in_=grouped)
+
+        def w1_quantize(g, u):
+            cols = slice(256 * u, 256 * u + 256)
+            quantize(w1_codes[g][:, cols], w1_scales[g][:, cols], w1_grp[g][:, 1024 * u : 1024 * u + 1024])
+
+        def w2_transpose(g, half, copy):
+            bank = ps_t.tile([P, 2, 256], F32, name="tr")
+            for u in range(2):
+                for jj in range(2):
+                    src = w_sb[:, 2 * half + jj, :].bitcast(F32)
+                    nc.tensor.transpose(
+                        bank[:, u, 128 * jj : 128 * jj + 128], src[:, 256 * g + u : 256 * g + 256 : 2], ident[:]
+                    )
+            dst = w2_grp[g][:, 256 * half : 256 * half + 256, :].rearrange("p c t -> p (c t)").bitcast(F32)
+            copy(out=dst.rearrange("p (c u) -> p c u", u=2), in_=bank[:].rearrange("p u c -> p c u"))
+
+        def w2_quantize(g):
+            quantize(w2_codes[g][:], w2_scales[g][:], w2_grp[g][:].rearrange("p c t -> p (c t)"))
+
+        x_grp, x_codes, x_scales, x_bank = {}, {}, {}, {}
+
+        def x_transpose(c, h):
+            b0, width = CHUNKS[c]
+            if h == 0:
+                x_grp[c] = xpool.tile([P, 512, 4], BF16, name="x_grp", align_bytes=64)
+                x_codes[c] = xpool.tile([P, 512], U32, name="x_codes", align_bytes=64)
+                x_scales[c] = xpool.tile([P, 512], U8, name="x_scales", align_bytes=64)
+            bank = ps_t.tile([P, 2, 256], F32, name="tr")
+            x_bank[c, h] = bank
+            for u in range(2):
+                for jj in range(2):
+                    src = x_sb[:, b0 // P + 2 * h + jj, :].bitcast(F32)
+                    nc.tensor.transpose(bank[:, u, 128 * jj : 128 * jj + 128], src[:, u:256:2], ident[:])
+
+        def x_multiply(c, h):
+            bank = x_bank[c, h]
+            raw = bank[:].rearrange("p u c -> p (u c)").bitcast(BF16)
+            nc.vector.tensor_tensor(
+                out=x_grp[c][:, 256 * h : 256 * h + 256, :].rearrange("p c (u e) -> p c u e", e=2),
+                in0=raw.rearrange("p (u c e) -> p c u e", u=2, e=2),
+                in1=a_bf[:].rearrange("p (u e) -> p u e", e=2).unsqueeze(1).to_broadcast([P, 256, 2, 2]),
+                op=ALU.mult,
+            )
+
+        def x_quantize(c):
+            width = CHUNKS[c][1]
+            quantize(
+                x_codes[c][:, :width],
+                x_scales[c][:, :width],
+                x_grp[c][:, :width, :].rearrange("p c t -> p (c t)"),
+            )
+
+        z_nat = {}
+
+        def label_factor(c, j):
+            b0, width = CHUNKS[c]
+            if j == 0:
+                z_nat[c] = xpool.tile([P, 4, N], BF16, name="z_nat")
+            nc.vector.tensor_scalar(
+                out=z_nat[c][:, j, :],
+                in0=y_sb[:, b0 // P + j, :],
+                scalar1=THRESHOLD,
+                scalar2=BETA,
+                op0=ALU.is_le,
+                op1=ALU.max,
+            )
+
+        units = [(c, g, u) for c in range(len(CHUNKS)) for g in range(2) for u in range(2)]
+        last_unit = {c: 4 * c + 3 for c in range(len(CHUNKS))}
+        z_bank, p_tile, d_tile, k_rows, k_grp, k_codes, k_scales = {}, {}, {}, {}, {}, {}, {}
+
+        def front(i):
+            c, g, u = units[i]
+            width = CHUNKS[c][1]
+            pt = kpool.tile([P, 2, 512], F32, name="pt", bufs=3)
+            p_tile[i] = pt
+            banks = []
+            for ee in range(2):
+                t = 2 * u + ee
+                if width == 512 or ee == 0:
+                    sb = ps_s.tile([P, 512], F32, name="sb")
+                cols = slice(0, width) if width == 512 else slice(256 * ee, 256 * ee + 256)
+                banks.append(sb[:, cols])
+                nc.tensor.matmul_mx(
+                    out=sb[:, cols],
+                    lhsT=w1_codes[g][:, P * t : P * t + P].bitcast(FP8X4),
+                    lhsT_scale=w1_scales[g][:, P * t : P * t + P],
+                    rhs=x_codes[c][:, :width].bitcast(FP8X4),
+                    rhs_scale=x_scales[c][:, :width],
+                    start=True,
+                    stop=True,
+                )
+            for ee in range(2):
+                t = 2 * u + ee
+                nc.scalar.activation(
+                    out=pt[:, ee, :width],
+                    in_=banks[ee],
+                    func=AF.Sigmoid,
+                    scale=e_32[:, g, t : t + 1],
+                    bias=b_32[:, g, t : t + 1],
+                )
+
+        def label_transpose(i):
+            c, g, u = units[i]
+            zb = ps_z.tile([P, 512], F32, name="zb")
+            z_bank[i] = zb
+            for j in range(CHUNKS[c][1] // P):
+                src = z_nat[c][:, j, :].bitcast(F32)
+                nc.tensor.transpose(zb[:, P * j : P * j + P], src[:, 256 * g + u : 256 * g + 256 : 2], ident[:])
+
+        def z_view(i):
+            width = CHUNKS[units[i][0]][1]
+            return z_bank[i][:, :width].bitcast(BF16).rearrange("p (c e) -> p e c", e=2)
+
+        def v1(i):
+            width = CHUNKS[units[i][0]][1]
+            dt = kpool.tile([P, 2, 512], F32, name="dt", bufs=3)
+            d_tile[i] = dt
+            nc.vector.scalar_tensor_tensor(
+                out=dt[:, :, :width],
+                in0=z_view(i),
+                scalar=0.9,
+                in1=p_tile[i][:, :, :width],
+                op0=ALU.is_lt,
+                op1=ALU.subtract,
+            )
+
+        def v2(i):
+            c, g, u = units[i]
+            width = CHUNKS[c][1]
+            if u == 0:
+                k_rows[c, g] = kpool.tile([P, 4, 512], BF16, name="k_rows", bufs=3)
+            zv = z_view(i)
+            for ee in range(2):
+                t = 2 * u + ee
+                nc.vector.scalar_tensor_tensor(
+                    out=k_rows[c, g][:, t, :width],
+                    in0=d_tile[i][:, ee, :width],
+                    scalar=ne_32[:, g, t : t + 1],
+                    in1=zv[:, ee, :],
+                    op0=ALU.mult,
+                    op1=ALU.mult,
+                )
+
+        def gcopy(out, in_):
+            nc.gpsimd.tensor_scalar(out=out, in0=in_, scalar1=1.0, scalar2=1.0, op0=ALU.mult, op1=ALU.mult)
+
+        def k_interleave(copy, c, g, lo, hi):
+            width = CHUNKS[c][1]
+            if lo == 0:
+                k_grp[c, g] = kpool.tile([P, 512, 4], BF16, name="k_grp", align_bytes=64)
+            cols = slice(lo * width // 16, hi * width // 16)
+            copy(out=k_grp[c, g][:, cols, :], in_=k_rows[c, g][:, :, cols].rearrange("p t c -> p c t"))
+
+        def k_quantize(c, g):
+            width = CHUNKS[c][1]
+            if g == 0:
+                k_codes[c] = kpool.tile([P, 2, 512], U32, name="k_codes", align_bytes=64)
+                k_scales[c] = kpool.tile([P, 2, 512], U8, name="k_scales", align_bytes=64)
+            quantize(
+                k_codes[c][:, g, :width],
+                k_scales[c][:, g, :width],
+                k_grp[c, g][:, :width, :].rearrange("p c t -> p (c t)"),
+            )
+
+        o_rows, p_grp, p_codes = {}, {}, {}
+        p_scales = const.tile([P, B], U8, align_bytes=64)
+
+        def scaled_copy_scalar(out, in_, t):
+            nc.scalar.activation(out=out, in_=in_, func=AF.Copy, scale=a_32[:, t : t + 1])
+
+        def scaled_copy_vector(out, in_, t):
+            nc.vector.tensor_scalar(out=out, in0=in_, scalar1=a_32[:, t : t + 1], scalar2=None, op0=ALU.mult)
+
+        def stage2(c, t, copy, pool, name):
+            width = CHUNKS[c][1]
+            if t == 0:
+                o_rows[c] = opool.tile([P, 4, 512], F32, name="o_rows")
+            ob = pool.tile([P, 512], F32, name=name)
+            for g in range(2):
+                nc.tensor.matmul_mx(
+                    out=ob[:, :width],
+                    lhsT=w2_codes[g][:, P * t : P * t + P].bitcast(FP8X4),
+                    lhsT_scale=w2_scales[g][:, P * t : P * t + P],
+                    rhs=k_codes[c][:, g, :width].bitcast(FP8X4),
+                    rhs_scale=k_scales[c][:, g, :width],
+                    start=(g == 0),
+                    stop=(g == 1),
+                )
+            copy(o_rows[c][:, t, :width], ob[:, :width], t)
+
+        def planes_group_gpsimd(c):
+            width = CHUNKS[c][1]
+            p_grp[c] = opool.tile([P, 512, 4], BF16, name="p_grp", align_bytes=64)
+            for b1 in range(0, width, 128):
+                cols = slice(b1, b1 + 128)
+                nc.gpsimd.tensor_scalar(
+                    out=p_grp[c][:, cols, :],
+                    in0=o_rows[c][:, :, cols].rearrange("p t c -> p c t"),
+                    scalar1=1.0,
+                    scalar2=1.0,
+                    op0=ALU.mult,
+                    op1=ALU.mult,
+                )
+
+        def planes_group_vector(c):
+            width = CHUNKS[c][1]
+            p_grp[c] = opool.tile([P, 512, 4], BF16, name="p_grp", align_bytes=64)
+            nc.vector.tensor_copy(
+                out=p_grp[c][:, :width, :], in_=o_rows[c][:, :, :width].rearrange("p t c -> p c t")
+            )
+
+        def planes_quantize(c):
+            b0, width = CHUNKS[c]
+            p_codes[c] = opool.tile([P, 512], U32, name="p_codes", align_bytes=64)
+            quantize(
+                p_codes[c][:, :width],
+                p_scales[:, b0 : b0 + width],
+                p_grp[c][:, :width, :].rearrange("p c t -> p (c t)"),
+            )
+            nc.sync.dma_start(
+                out=words_out[:, b0 : b0 + width], in_=p_codes[c][:, :width].bitcast(I32)
+            )
+
+        def scales_store(b0, b1):
+            for q in range(4):
+                nc.sync.dma_start(
+                    out=scales_out[4 * q : 4 * q + 4, b0 // 4 : b1 // 4],
+                    in_=p_scales[32 * q : 32 * q + 4, b0:b1].bitcast(I32),
+                )
+
+        def out_tile(c, j, copy):
+            b0, width = CHUNKS[c]
+            bank = ps_t.tile([P, 4, P], F32, name="tr")
+            for t in range(4):
+                nc.tensor.transpose(bank[:, t, :], o_rows[c][:, t, P * j : P * j + P], ident[:])
+            row = opool.tile([P, D], F32, name="out_row", bufs=3)
+            copy(out=row[:].rearrange("c (m t) -> c m t", t=4), in_=bank[:].rearrange("c t m -> c m t"))
+            nc.sync.dma_start(out=out_0[b0 + P * j : b0 + P * j + P, :], in_=row[:])
+
+        mid, post, actx = {}, {}, {}
+
+        def add(table, step, *call):
+            table.setdefault(step, []).append(call)
+
+        def emit(table, step):
+            for call in table.get(step, []):
+                call[0](*call[1:])
+
+        scopy, vcopy = nc.scalar.copy, nc.vector.tensor_copy
+        n_chunks = len(CHUNKS)
+        GS = 11
+        for c in range(n_chunks):
+            width = CHUNKS[c][1]
+            last = last_unit[c]
+            tail = c == n_chunks - 1
+            add(post, last - 2, k_interleave, scopy, c, 0, 0, 6)
+            add(post, last - 2, k_interleave, gcopy, c, 0, GS, 16)
+            add(actx, last - 1, k_interleave, scopy, c, 0, 6, GS)
+            add(mid, last, k_quantize, c, 0)
+            if tail:
+                add(post, last, k_interleave, scopy, c, 1, 0, 6)
+                add(post, last, k_interleave, vcopy, c, 1, 6, 16)
+                add(post, last, k_quantize, c, 1)
+                for t in range(4):
+                    copy = scaled_copy_scalar if t % 2 == 0 else scaled_copy_vector
+                    add(post, last + 3, stage2, c, t, copy, ps_s if t > 1 else ps_z, "sb" if t > 1 else "zb")
+                add(post, last + 4, planes_group_vector, c)
+                for j in range(width // P):
+                    add(post, last + 5, out_tile, c, j, scopy if j % 2 == 0 else vcopy)
+                add(post, last + 6, planes_quantize, c)
+                add(post, last + 6, scales_store, CHUNKS[c][0], B)
+            else:
+                add(post, last, k_interleave, scopy, c, 1, 0, 6)
+                add(post, last, k_interleave, gcopy, c, 1, GS, 16)
+                add(actx, last + 1, k_interleave, scopy, c, 1, 6, GS)
+                add(mid, last + 2, k_quantize, c, 1)
+                for t in range(4):
+                    add(actx, last + 3 + t // 2, stage2, c, t, scaled_copy_scalar, ps_t, "tr")
+                add(post, last + 4, planes_group_gpsimd, c)
+                for j in range(width // P):
+                    add(actx, last + 5 + j // 2, out_tile, c, j, scopy)
+                add(mid, last + 7, planes_quantize, c)
+                if c == n_chunks - 2:
+                    add(mid, last + 7, scales_store, 0, CHUNKS[-1][0])
+            if c > 1:
+                first = 4 * c
+                for j in range(width // P):
+                    add(mid, first - 6 + j, label_factor, c, j)
+                for h in range(width // 256):
+                    add(actx, first - 6 + h, x_transpose, c, h)
+                    add(mid, first - 5 + h, x_multiply, c, h)
+                add(mid, first - 3, x_quantize, c)
+        for h in range(2):
+            add(actx, h - 1, x_transpose, 1, h)
+            add(mid, h, x_multiply, 1, h)
+        for j in range(4):
+            add(mid, j // 2, label_factor, 1, j)
+        add(mid, 1, x_quantize, 1)
+        add(actx, 1, w2_transpose, 0, 0, scopy)
+        add(actx, 1, w2_transpose, 0, 1, scopy)
+        add(actx, 2, w2_transpose, 1, 0, scopy)
+        add(actx, 2, w2_transpose, 1, 1, scopy)
+        add(mid, 3, w2_quantize, 0)
+        add(mid, 4, w2_quantize, 1)
+
+        x_transpose(0, 0)
+        x_multiply(0, 0)
+        x_quantize(0)
+        w1_interleave(scopy, 0, 1)
+        w1_interleave(vcopy, 0, 0)
+        constants()
+        w1_quantize(0, 0)
+        label_factor(0, 0)
+        label_factor(0, 1)
+        front(0)
+        label_transpose(0)
+        w1_quantize(0, 1)
+        front(1)
+        label_transpose(1)
+        w1_interleave(scopy, 1, 1)
+        w1_interleave(vcopy, 1, 0)
+        v1(0)
+        emit(mid, -1)
+        emit(actx, -1)
+        emit(post, -1)
+        w1_quantize(1, 0)
+        w1_quantize(1, 1)
+        n_units = len(units)
+        for i in range(n_units + 8):
+            if i + 2 < n_units:
+                front(i + 2)
+            emit(actx, i)
+            if i + 2 < n_units:
+                label_transpose(i + 2)
+            if i + 1 < n_units:
+                v1(i + 1)
+            emit(mid, i)
+            if i < n_units:
+                v2(i)
+            emit(post, i)

@@ -18,6 +18,7 @@ FP8X4 = mybir.dt.float8_e4m3fn_x4
 ALU = mybir.AluOpType
 AF = mybir.ActivationFunctionType
 
+S = {'r': {'eng': ['gss', 'gss'], 'gs': [4, 3], 'hs': [8, 11], 'ilg': [['post', 0], ['actx', 1]], 'ila': [['mid', 2], ['mid', 1]], 'ilb': [['mid', 1], ['mid', 1]], 'kq': [['post', 2], ['mid', 3]], 'st': [['actx', 4], ['actx', 4], ['actx', 5], ['actx', 5]], 'oce': 'ssss', 'pg': ['mid', 6], 'pge': 'g', 'ot': [['mid', 6], ['actx', 6], ['actx', 7], ['actx', 7]], 'ote': 'ssss', 'pq': ['post', 7]}, 'q': {'eng': ['ggs', 'gss'], 'gs': [4, 5], 'hs': [10, 10], 'ilg': [['post', 0], ['actx', 1]], 'ila': [['actx', 2], ['actx', 1]], 'ilb': [['mid', 1], ['post', 1]], 'kq': [['post', 2], ['actx', 2]], 'st': [['actx', 3], ['mid', 3], ['actx', 4], ['post', 4]], 'oce': 'ssss'}, 't': {'eng': ['vvg'], 'gs': [1], 'hs': [6], 'ilg': [['actx', 1]], 'ila': [['post', 1]], 'ilb': [['actx', 1]], 'kq': [['post', 2]]}, 'tl': 3, 'we': 'v', 'lf0': ['post', -6], 'lf1': ['post', -5], 'lf2': ['mid', -3], 'lf3': ['actx', -2], 'xt0': ['actx', -6], 'xt1': ['actx', -4], 'xm0': ['actx', -5], 'xm1': ['actx', -4], 'xq': ['actx', -3], 'hxt0': ['actx', -1], 'hxt1': ['post', -1], 'hxm0': ['post', -1], 'hxm1': ['post', -1], 'hlf0': ['mid', -1], 'hlf1': ['mid', 0], 'hlf2': ['post', 1], 'hlf3': ['actx', 1], 'hxq': ['actx', 1], 'wt0': ['actx', 5], 'wt1': ['actx', 5], 'wt2': ['mid', 4], 'wt3': ['actx', 1], 'wq0': ['mid', 5], 'wq1': ['actx', 5]}
 CHUNKS = [(0, 256), (256, 512), (768, 512), (1280, 512), (1792, 256)]
 
 
@@ -141,17 +142,18 @@ def tile_gbcecandidatelossusergradient_x1_kernel(tc, x, a, w, e, b, y, out_0, ou
             bank = ps_t.tile([P, 2, 256], F32, name="tr")
             x_bank[c, h] = bank
             for u in range(2):
-                for jj in range(2):
+                for jj in range(min(2, width // P)):
                     src = x_sb[:, b0 // P + 2 * h + jj, :].bitcast(F32)
                     nc.tensor.transpose(bank[:, u, 128 * jj : 128 * jj + 128], src[:, u:256:2], ident[:])
 
         def x_multiply(c, h):
             bank = x_bank[c, h]
-            raw = bank[:].rearrange("p u c -> p (u c)").bitcast(BF16)
+            cols = min(256, CHUNKS[c][1])
+            raw = bank[:].rearrange("p u c -> p (u c)").bitcast(BF16).rearrange("p (u c e) -> p c u e", u=2, e=2)
             nc.vector.tensor_tensor(
-                out=x_grp[c][:, 256 * h : 256 * h + 256, :].rearrange("p c (u e) -> p c u e", e=2),
-                in0=raw.rearrange("p (u c e) -> p c u e", u=2, e=2),
-                in1=a_bf[:].rearrange("p (u e) -> p u e", e=2).unsqueeze(1).to_broadcast([P, 256, 2, 2]),
+                out=x_grp[c][:, 256 * h : 256 * h + cols, :].rearrange("p c (u e) -> p c u e", e=2),
+                in0=raw[:, :cols, :, :],
+                in1=a_bf[:].rearrange("p (u e) -> p u e", e=2).unsqueeze(1).to_broadcast([P, cols, 2, 2]),
                 op=ALU.mult,
             )
 
@@ -192,7 +194,7 @@ def tile_gbcecandidatelossusergradient_x1_kernel(tc, x, a, w, e, b, y, out_0, ou
                 t = 2 * u + ee
                 if width == 512 or ee == 0:
                     sb = ps_s.tile([P, 512], F32, name="sb")
-                cols = slice(0, width) if width == 512 else slice(256 * ee, 256 * ee + 256)
+                cols = slice(0, width) if width == 512 else slice(width * ee, width * ee + width)
                 banks.append(sb[:, cols])
                 nc.tensor.matmul_mx(
                     out=sb[:, cols],
@@ -347,75 +349,60 @@ def tile_gbcecandidatelossusergradient_x1_kernel(tc, x, a, w, e, b, y, out_0, ou
             bank = ps_t.tile([P, 4, P], F32, name="tr")
             for t in range(4):
                 nc.tensor.transpose(bank[:, t, :], o_rows[c][:, t, P * j : P * j + P], ident[:])
-            row = opool.tile([P, D], F32, name="out_row", bufs=3)
+            row = opool.tile([P, D], F32, name="out_row", bufs=6)
             copy(out=row[:].rearrange("c (m t) -> c m t", t=4), in_=bank[:].rearrange("c t m -> c m t"))
             nc.sync.dma_start(out=out_0[b0 + P * j : b0 + P * j + P, :], in_=row[:])
 
-        mid, post, actx = {}, {}, {}
+        tables = {"actx": {}, "mid": {}, "post": {}}
 
-        def add(table, step, *call):
-            table.setdefault(step, []).append(call)
+        def add(place, base, *call):
+            tables[place[0]].setdefault(base + place[1], []).append(call)
 
         def emit(table, step):
-            for call in table.get(step, []):
+            for call in tables[table].get(step, []):
                 call[0](*call[1:])
 
         scopy, vcopy = nc.scalar.copy, nc.vector.tensor_copy
+        copiers = {"s": scopy, "v": vcopy, "g": gcopy}
+        scalers = {"s": scaled_copy_scalar, "v": scaled_copy_vector}
+        groupers = {"g": planes_group_gpsimd, "v": planes_group_vector}
         n_chunks = len(CHUNKS)
-        GS = 11
         for c in range(n_chunks):
-            width = CHUNKS[c][1]
+            b0, width = CHUNKS[c]
             last = last_unit[c]
-            tail = c == n_chunks - 1
-            add(post, last - 2, k_interleave, scopy, c, 0, 0, 6)
-            add(post, last - 2, k_interleave, gcopy, c, 0, GS, 16)
-            add(actx, last - 1, k_interleave, scopy, c, 0, 6, GS)
-            add(mid, last, k_quantize, c, 0)
-            if tail:
-                add(post, last, k_interleave, scopy, c, 1, 0, 6)
-                add(post, last, k_interleave, vcopy, c, 1, 6, 16)
-                add(post, last, k_quantize, c, 1)
+            R = S["r"] if c < n_chunks - 2 else S["q"] if c == n_chunks - 2 else S["t"]
+            for g in range(2 if c < n_chunks - 1 else 1):
+                base = last - 2 + 2 * g
+                add(R["ilg"][g], base, k_interleave, copiers[R["eng"][g][0]], c, g, 0, R["gs"][g])
+                add(R["ila"][g], base, k_interleave, copiers[R["eng"][g][1]], c, g, R["gs"][g], R["hs"][g])
+                add(R["ilb"][g], base, k_interleave, copiers[R["eng"][g][2]], c, g, R["hs"][g], 16)
+                add(R["kq"][g], base, k_quantize, c, g)
+            if c < n_chunks - 1:
                 for t in range(4):
-                    copy = scaled_copy_scalar if t % 2 == 0 else scaled_copy_vector
-                    add(post, last + 3, stage2, c, t, copy, ps_s if t > 1 else ps_z, "sb" if t > 1 else "zb")
-                add(post, last + 4, planes_group_vector, c)
+                    add(R["st"][t], last, stage2, c, t, scalers[R["oce"][t]], ps_t, "tr")
+            if c < n_chunks - 2:
+                add(R["pg"], last, groupers[R["pge"]], c)
                 for j in range(width // P):
-                    add(post, last + 5, out_tile, c, j, scopy if j % 2 == 0 else vcopy)
-                add(post, last + 6, planes_quantize, c)
-                add(post, last + 6, scales_store, CHUNKS[c][0], B)
-            else:
-                add(post, last, k_interleave, scopy, c, 1, 0, 6)
-                add(post, last, k_interleave, gcopy, c, 1, GS, 16)
-                add(actx, last + 1, k_interleave, scopy, c, 1, 6, GS)
-                add(mid, last + 2, k_quantize, c, 1)
-                for t in range(4):
-                    add(actx, last + 3 + t // 2, stage2, c, t, scaled_copy_scalar, ps_t, "tr")
-                add(post, last + 4, planes_group_gpsimd, c)
-                for j in range(width // P):
-                    add(actx, last + 5 + j // 2, out_tile, c, j, scopy)
-                add(mid, last + 7, planes_quantize, c)
-                if c == n_chunks - 2:
-                    add(mid, last + 7, scales_store, 0, CHUNKS[-1][0])
+                    add(R["ot"][j], last, out_tile, c, j, copiers[R["ote"][j]])
+                add(R["pq"], last, planes_quantize, c)
             if c > 1:
                 first = 4 * c
                 for j in range(width // P):
-                    add(mid, first - 6 + j, label_factor, c, j)
-                for h in range(width // 256):
-                    add(actx, first - 6 + h, x_transpose, c, h)
-                    add(mid, first - 5 + h, x_multiply, c, h)
-                add(mid, first - 3, x_quantize, c)
+                    add(S["lf%d" % j], first, label_factor, c, j)
+                for h in range(max(1, width // 256)):
+                    add(S["xt%d" % h], first, x_transpose, c, h)
+                    add(S["xm%d" % h], first, x_multiply, c, h)
+                add(S["xq"], first, x_quantize, c)
         for h in range(2):
-            add(actx, h - 1, x_transpose, 1, h)
-            add(mid, h, x_multiply, 1, h)
+            add(S["hxt%d" % h], 0, x_transpose, 1, h)
+            add(S["hxm%d" % h], 0, x_multiply, 1, h)
         for j in range(4):
-            add(mid, j // 2, label_factor, 1, j)
-        add(mid, 1, x_quantize, 1)
-        add(actx, 1, w2_transpose, 0, 0, scopy)
-        add(actx, 1, w2_transpose, 0, 1, scopy)
-        add(actx, 2, w2_transpose, 1, 0, scopy)
-        add(actx, 2, w2_transpose, 1, 1, scopy)
-        add(mid, 3, w2_quantize, 0)
-        add(mid, 4, w2_quantize, 1)
+            add(S["hlf%d" % j], 0, label_factor, 1, j)
+        add(S["hxq"], 0, x_quantize, 1)
+        for q in range(4):
+            add(S["wt%d" % q], 0, w2_transpose, q // 2, q % 2, scopy)
+        add(S["wq0"], 0, w2_quantize, 0)
+        add(S["wq1"], 0, w2_quantize, 1)
 
         x_transpose(0, 0)
         x_multiply(0, 0)
@@ -432,23 +419,42 @@ def tile_gbcecandidatelossusergradient_x1_kernel(tc, x, a, w, e, b, y, out_0, ou
         front(1)
         label_transpose(1)
         w1_interleave(scopy, 1, 1)
-        w1_interleave(vcopy, 1, 0)
+        w1_interleave(copiers[S["we"]], 1, 0)
         v1(0)
-        emit(mid, -1)
-        emit(actx, -1)
-        emit(post, -1)
+        emit("mid", -1)
+        emit("actx", -1)
+        emit("post", -1)
         w1_quantize(1, 0)
         w1_quantize(1, 1)
         n_units = len(units)
-        for i in range(n_units + 8):
+        for i in range(n_units):
             if i + 2 < n_units:
                 front(i + 2)
-            emit(actx, i)
+            emit("actx", i)
             if i + 2 < n_units:
                 label_transpose(i + 2)
             if i + 1 < n_units:
                 v1(i + 1)
-            emit(mid, i)
+            emit("mid", i)
             if i < n_units:
                 v2(i)
-            emit(post, i)
+            emit("post", i)
+
+        c = n_chunks - 1
+        k_interleave(scopy, c, 1, 0, S["tl"])
+        k_interleave(vcopy, c, 1, S["tl"], 16)
+        k_quantize(c, 1)
+        planes_group_gpsimd(c - 1)
+        out_tile(c - 1, 0, scopy)
+        out_tile(c - 1, 1, vcopy)
+        out_tile(c - 1, 2, scopy)
+        for t in range(4):
+            stage2(c, t, scaled_copy_scalar if t % 2 == 0 else scaled_copy_vector, ps_s, "sb")
+        out_tile(c - 1, 3, vcopy)
+        planes_quantize(c - 1)
+        scales_store(0, CHUNKS[c][0])
+        out_tile(c, 0, scopy)
+        out_tile(c, 1, vcopy)
+        planes_group_vector(c)
+        planes_quantize(c)
+        scales_store(CHUNKS[c][0], B)

from contextlib import ExitStack

import concourse.mybir as mybir
from concourse.masks import make_identity

B, D, N = 2048, 512, 1024
BETA = 0.625
THRESHOLD = 0.8
FLOPS = 4 * B * D * N

P = 128
F32 = mybir.dt.float32
BF16 = mybir.dt.bfloat16
I32 = mybir.dt.int32
U32 = mybir.dt.uint32
U8 = mybir.dt.uint8
FP8X4 = mybir.dt.float8_e4m3fn_x4
ALU = mybir.AluOpType
AF = mybir.ActivationFunctionType

S = {'r': {'eng': ['gss', 'gss'], 'gs': [4, 3], 'hs': [8, 11], 'ilg': [['post', 0], ['actx', 1]], 'ila': [['mid', 2], ['mid', 1]], 'ilb': [['mid', 1], ['mid', 1]], 'kq': [['post', 2], ['mid', 3]], 'st': [['actx', 4], ['actx', 4], ['actx', 5], ['actx', 5]], 'oce': 'ssss', 'pg': ['mid', 6], 'pge': 'g', 'ot': [['mid', 6], ['actx', 6], ['actx', 7], ['actx', 7]], 'ote': 'ssss', 'pq': ['post', 7]}, 'q': {'eng': ['ggs', 'gss'], 'gs': [4, 5], 'hs': [10, 10], 'ilg': [['post', 0], ['actx', 1]], 'ila': [['actx', 2], ['actx', 1]], 'ilb': [['mid', 1], ['post', 1]], 'kq': [['post', 2], ['actx', 2]], 'st': [['actx', 3], ['mid', 3], ['actx', 4], ['post', 4]], 'oce': 'ssss'}, 't': {'eng': ['vvg'], 'gs': [1], 'hs': [6], 'ilg': [['actx', 1]], 'ila': [['post', 1]], 'ilb': [['actx', 1]], 'kq': [['post', 2]]}, 'tl': 3, 'we': 'v', 'lf0': ['post', -6], 'lf1': ['post', -5], 'lf2': ['mid', -3], 'lf3': ['actx', -2], 'xt0': ['actx', -6], 'xt1': ['actx', -4], 'xm0': ['actx', -5], 'xm1': ['actx', -4], 'xq': ['actx', -3], 'hxt0': ['actx', -1], 'hxt1': ['post', -1], 'hxm0': ['post', -1], 'hxm1': ['post', -1], 'hlf0': ['mid', -1], 'hlf1': ['mid', 0], 'hlf2': ['post', 1], 'hlf3': ['actx', 1], 'hxq': ['actx', 1], 'wt0': ['actx', 5], 'wt1': ['actx', 5], 'wt2': ['mid', 4], 'wt3': ['actx', 1], 'wq0': ['mid', 5], 'wq1': ['actx', 5]}
CHUNKS = [(0, 256), (256, 512), (768, 512), (1280, 512), (1792, 256)]


def tile_gbcecandidatelossusergradient_x1_kernel(tc, x, a, w, e, b, y, out_0, out_1, out_2):
    nc = tc.nc
    words_out = out_1.rearrange("g p m t -> (g p) (m t)").bitcast(I32)
    scales_out = out_2.rearrange("g q m -> (g q) m").bitcast(I32)

    with ExitStack() as ctx:
        const = ctx.enter_context(tc.tile_pool(name="const", bufs=1))
        xpool = ctx.enter_context(tc.tile_pool(name="xpool", bufs=2))
        kpool = ctx.enter_context(tc.tile_pool(name="kpool", bufs=2))
        opool = ctx.enter_context(tc.tile_pool(name="opool", bufs=2))
        ps_s = ctx.enter_context(tc.psum_pool(name="ps_s", bufs=2))
        ps_z = ctx.enter_context(tc.psum_pool(name="ps_z", bufs=3))
        ps_t = ctx.enter_context(tc.psum_pool(name="ps_t", bufs=3))
        ctx.enter_context(tc.manual_schedule())

        x_sb = const.tile([P, B // P, D], BF16)
        y_sb = const.tile([P, B // P, N], BF16)
        w_sb = const.tile([P, 4, N], BF16)
        a_bf = const.tile([P, 4], BF16)
        e_bf = const.tile([P, 2, 4], BF16)
        b_bf = const.tile([P, 2, 4], BF16)
        nc.scalar.dma_start(out=a_bf[:], in_=a.rearrange("(p t) -> p t", t=4))
        nc.scalar.dma_start(out=e_bf[:], in_=e.rearrange("(g p t) -> p g t", g=2, t=4))
        nc.scalar.dma_start(out=b_bf[:], in_=b.rearrange("(g p t) -> p g t", g=2, t=4))

        def load_x(c):
            b0, width = CHUNKS[c]
            nc.sync.dma_start(
                out=x_sb[:, b0 // P : (b0 + width) // P, :],
                in_=x[b0 : b0 + width, :].rearrange("(j p) d -> p j d", p=P),
            )

        def load_y(b0, width):
            nc.sync.dma_start(
                out=y_sb[:, b0 // P : (b0 + width) // P, :],
                in_=y[b0 : b0 + width, :].rearrange("(j p) n -> p j n", p=P),
            )

        def load_w(g):
            nc.sync.dma_start(
                out=w_sb[:, :, 512 * g : 512 * g + 512],
                in_=w[:, 512 * g : 512 * g + 512].rearrange("(p j) n -> p j n", j=4),
            )

        load_x(0)
        load_w(0)
        load_y(0, 256)
        load_w(1)
        load_x(1)
        load_y(256, 256)
        load_y(512, 256)
        load_x(2)
        load_y(768, 512)
        load_x(3)
        load_y(1280, 512)
        load_x(4)
        load_y(1792, 256)

        ident = const.tile([P, P], F32)
        make_identity(nc, ident[:])
        warm = const.tile([P, 1], F32)
        nc.vector.memset(warm[:], 0.0)
        warm_out = const.tile([P, 1], F32)
        nc.scalar.activation(out=warm_out[:], in_=warm[:], func=AF.Sigmoid)

        a_32 = const.tile([P, 4], F32)
        e_32 = const.tile([P, 2, 4], F32)
        ne_32 = const.tile([P, 2, 4], F32)
        b_32 = const.tile([P, 2, 4], F32)

        def constants():
            nc.vector.tensor_copy(out=e_32[:], in_=e_bf[:])
            nc.vector.tensor_copy(out=b_32[:], in_=b_bf[:])
            nc.vector.tensor_scalar(out=ne_32[:], in0=e_bf[:], scalar1=-1.0, scalar2=None, op0=ALU.mult)
            nc.vector.tensor_copy(out=a_32[:], in_=a_bf[:])

        w1_grp = [const.tile([P, 2048], BF16, name="w1_grp%d" % g, align_bytes=64) for g in range(2)]
        w1_codes = [const.tile([P, 512], U32, name="w1_codes%d" % g, align_bytes=64) for g in range(2)]
        w1_scales = [const.tile([P, 512], U8, name="w1_scales%d" % g, align_bytes=64) for g in range(2)]
        w2_grp = [const.tile([P, 512, 4], BF16, name="w2_grp%d" % g, align_bytes=64) for g in range(2)]
        w2_codes = [const.tile([P, 512], U32, name="w2_codes%d" % g, align_bytes=64) for g in range(2)]
        w2_scales = [const.tile([P, 512], U8, name="w2_scales%d" % g, align_bytes=64) for g in range(2)]

        def w1_interleave(copy, g, u):
            dst = w1_grp[g][:, 1024 * u : 1024 * u + 1024].rearrange("p (t m j) -> p t m j", t=2, j=4)
            src = w_sb[:, :, 512 * g : 512 * g + 512].rearrange("p j (m t) -> p t m j", t=4)
            copy(out=dst, in_=src[:, 2 * u : 2 * u + 2, :, :])

        def quantize(codes, scales, grouped):
            nc.vector.quantize_mx(out=codes.bitcast(FP8X4), scales=scales, in_=grouped)

        def w1_quantize(g, u):
            cols = slice(256 * u, 256 * u + 256)
            quantize(w1_codes[g][:, cols], w1_scales[g][:, cols], w1_grp[g][:, 1024 * u : 1024 * u + 1024])

        def w2_transpose(g, half, copy):
            bank = ps_t.tile([P, 2, 256], F32, name="tr")
            for u in range(2):
                for jj in range(2):
                    src = w_sb[:, 2 * half + jj, :].bitcast(F32)
                    nc.tensor.transpose(
                        bank[:, u, 128 * jj : 128 * jj + 128], src[:, 256 * g + u : 256 * g + 256 : 2], ident[:]
                    )
            dst = w2_grp[g][:, 256 * half : 256 * half + 256, :].rearrange("p c t -> p (c t)").bitcast(F32)
            copy(out=dst.rearrange("p (c u) -> p c u", u=2), in_=bank[:].rearrange("p u c -> p c u"))

        def w2_quantize(g):
            quantize(w2_codes[g][:], w2_scales[g][:], w2_grp[g][:].rearrange("p c t -> p (c t)"))

        x_grp, x_codes, x_scales, x_bank = {}, {}, {}, {}

        def x_transpose(c, h):
            b0, width = CHUNKS[c]
            if h == 0:
                x_grp[c] = xpool.tile([P, 512, 4], BF16, name="x_grp", align_bytes=64)
                x_codes[c] = xpool.tile([P, 512], U32, name="x_codes", align_bytes=64)
                x_scales[c] = xpool.tile([P, 512], U8, name="x_scales", align_bytes=64)
            bank = ps_t.tile([P, 2, 256], F32, name="tr")
            x_bank[c, h] = bank
            for u in range(2):
                for jj in range(min(2, width // P)):
                    src = x_sb[:, b0 // P + 2 * h + jj, :].bitcast(F32)
                    nc.tensor.transpose(bank[:, u, 128 * jj : 128 * jj + 128], src[:, u:256:2], ident[:])

        def x_multiply(c, h):
            bank = x_bank[c, h]
            cols = min(256, CHUNKS[c][1])
            raw = bank[:].rearrange("p u c -> p (u c)").bitcast(BF16).rearrange("p (u c e) -> p c u e", u=2, e=2)
            nc.vector.tensor_tensor(
                out=x_grp[c][:, 256 * h : 256 * h + cols, :].rearrange("p c (u e) -> p c u e", e=2),
                in0=raw[:, :cols, :, :],
                in1=a_bf[:].rearrange("p (u e) -> p u e", e=2).unsqueeze(1).to_broadcast([P, cols, 2, 2]),
                op=ALU.mult,
            )

        def x_quantize(c):
            width = CHUNKS[c][1]
            quantize(
                x_codes[c][:, :width],
                x_scales[c][:, :width],
                x_grp[c][:, :width, :].rearrange("p c t -> p (c t)"),
            )

        z_nat = {}

        def label_factor(c, j):
            b0, width = CHUNKS[c]
            if j == 0:
                z_nat[c] = xpool.tile([P, 4, N], BF16, name="z_nat")
            nc.vector.tensor_scalar(
                out=z_nat[c][:, j, :],
                in0=y_sb[:, b0 // P + j, :],
                scalar1=THRESHOLD,
                scalar2=BETA,
                op0=ALU.is_le,
                op1=ALU.max,
            )

        units = [(c, g, u) for c in range(len(CHUNKS)) for g in range(2) for u in range(2)]
        last_unit = {c: 4 * c + 3 for c in range(len(CHUNKS))}
        z_bank, p_tile, d_tile, k_rows, k_grp, k_codes, k_scales = {}, {}, {}, {}, {}, {}, {}

        def front(i):
            c, g, u = units[i]
            width = CHUNKS[c][1]
            pt = kpool.tile([P, 2, 512], F32, name="pt", bufs=3)
            p_tile[i] = pt
            banks = []
            for ee in range(2):
                t = 2 * u + ee
                if width == 512 or ee == 0:
                    sb = ps_s.tile([P, 512], F32, name="sb")
                cols = slice(0, width) if width == 512 else slice(width * ee, width * ee + width)
                banks.append(sb[:, cols])
                nc.tensor.matmul_mx(
                    out=sb[:, cols],
                    lhsT=w1_codes[g][:, P * t : P * t + P].bitcast(FP8X4),
                    lhsT_scale=w1_scales[g][:, P * t : P * t + P],
                    rhs=x_codes[c][:, :width].bitcast(FP8X4),
                    rhs_scale=x_scales[c][:, :width],
                    start=True,
                    stop=True,
                )
            for ee in range(2):
                t = 2 * u + ee
                nc.scalar.activation(
                    out=pt[:, ee, :width],
                    in_=banks[ee],
                    func=AF.Sigmoid,
                    scale=e_32[:, g, t : t + 1],
                    bias=b_32[:, g, t : t + 1],
                )

        def label_transpose(i):
            c, g, u = units[i]
            zb = ps_z.tile([P, 512], F32, name="zb")
            z_bank[i] = zb
            for j in range(CHUNKS[c][1] // P):
                src = z_nat[c][:, j, :].bitcast(F32)
                nc.tensor.transpose(zb[:, P * j : P * j + P], src[:, 256 * g + u : 256 * g + 256 : 2], ident[:])

        def z_view(i):
            width = CHUNKS[units[i][0]][1]
            return z_bank[i][:, :width].bitcast(BF16).rearrange("p (c e) -> p e c", e=2)

        def v1(i):
            width = CHUNKS[units[i][0]][1]
            dt = kpool.tile([P, 2, 512], F32, name="dt", bufs=3)
            d_tile[i] = dt
            nc.vector.scalar_tensor_tensor(
                out=dt[:, :, :width],
                in0=z_view(i),
                scalar=0.9,
                in1=p_tile[i][:, :, :width],
                op0=ALU.is_lt,
                op1=ALU.subtract,
            )

        def v2(i):
            c, g, u = units[i]
            width = CHUNKS[c][1]
            if u == 0:
                k_rows[c, g] = kpool.tile([P, 4, 512], BF16, name="k_rows", bufs=3)
            zv = z_view(i)
            for ee in range(2):
                t = 2 * u + ee
                nc.vector.scalar_tensor_tensor(
                    out=k_rows[c, g][:, t, :width],
                    in0=d_tile[i][:, ee, :width],
                    scalar=ne_32[:, g, t : t + 1],
                    in1=zv[:, ee, :],
                    op0=ALU.mult,
                    op1=ALU.mult,
                )

        def gcopy(out, in_):
            nc.gpsimd.tensor_scalar(out=out, in0=in_, scalar1=1.0, scalar2=1.0, op0=ALU.mult, op1=ALU.mult)

        def k_interleave(copy, c, g, lo, hi):
            width = CHUNKS[c][1]
            if lo == 0:
                k_grp[c, g] = kpool.tile([P, 512, 4], BF16, name="k_grp", align_bytes=64)
            cols = slice(lo * width // 16, hi * width // 16)
            copy(out=k_grp[c, g][:, cols, :], in_=k_rows[c, g][:, :, cols].rearrange("p t c -> p c t"))

        def k_quantize(c, g):
            width = CHUNKS[c][1]
            if g == 0:
                k_codes[c] = kpool.tile([P, 2, 512], U32, name="k_codes", align_bytes=64)
                k_scales[c] = kpool.tile([P, 2, 512], U8, name="k_scales", align_bytes=64)
            quantize(
                k_codes[c][:, g, :width],
                k_scales[c][:, g, :width],
                k_grp[c, g][:, :width, :].rearrange("p c t -> p (c t)"),
            )

        o_rows, p_grp, p_codes = {}, {}, {}
        p_scales = const.tile([P, B], U8, align_bytes=64)

        def scaled_copy_scalar(out, in_, t):
            nc.scalar.activation(out=out, in_=in_, func=AF.Copy, scale=a_32[:, t : t + 1])

        def scaled_copy_vector(out, in_, t):
            nc.vector.tensor_scalar(out=out, in0=in_, scalar1=a_32[:, t : t + 1], scalar2=None, op0=ALU.mult)

        def stage2(c, t, copy, pool, name):
            width = CHUNKS[c][1]
            if t == 0:
                o_rows[c] = opool.tile([P, 4, 512], F32, name="o_rows")
            ob = pool.tile([P, 512], F32, name=name)
            for g in range(2):
                nc.tensor.matmul_mx(
                    out=ob[:, :width],
                    lhsT=w2_codes[g][:, P * t : P * t + P].bitcast(FP8X4),
                    lhsT_scale=w2_scales[g][:, P * t : P * t + P],
                    rhs=k_codes[c][:, g, :width].bitcast(FP8X4),
                    rhs_scale=k_scales[c][:, g, :width],
                    start=(g == 0),
                    stop=(g == 1),
                )
            copy(o_rows[c][:, t, :width], ob[:, :width], t)

        def planes_group_gpsimd(c):
            width = CHUNKS[c][1]
            p_grp[c] = opool.tile([P, 512, 4], BF16, name="p_grp", align_bytes=64)
            for b1 in range(0, width, 128):
                cols = slice(b1, b1 + 128)
                nc.gpsimd.tensor_scalar(
                    out=p_grp[c][:, cols, :],
                    in0=o_rows[c][:, :, cols].rearrange("p t c -> p c t"),
                    scalar1=1.0,
                    scalar2=1.0,
                    op0=ALU.mult,
                    op1=ALU.mult,
                )

        def planes_group_vector(c):
            width = CHUNKS[c][1]
            p_grp[c] = opool.tile([P, 512, 4], BF16, name="p_grp", align_bytes=64)
            nc.vector.tensor_copy(
                out=p_grp[c][:, :width, :], in_=o_rows[c][:, :, :width].rearrange("p t c -> p c t")
            )

        def planes_quantize(c):
            b0, width = CHUNKS[c]
            p_codes[c] = opool.tile([P, 512], U32, name="p_codes", align_bytes=64)
            quantize(
                p_codes[c][:, :width],
                p_scales[:, b0 : b0 + width],
                p_grp[c][:, :width, :].rearrange("p c t -> p (c t)"),
            )
            nc.sync.dma_start(
                out=words_out[:, b0 : b0 + width], in_=p_codes[c][:, :width].bitcast(I32)
            )

        def scales_store(b0, b1):
            for q in range(4):
                nc.sync.dma_start(
                    out=scales_out[4 * q : 4 * q + 4, b0 // 4 : b1 // 4],
                    in_=p_scales[32 * q : 32 * q + 4, b0:b1].bitcast(I32),
                )

        def out_tile(c, j, copy):
            b0, width = CHUNKS[c]
            bank = ps_t.tile([P, 4, P], F32, name="tr")
            for t in range(4):
                nc.tensor.transpose(bank[:, t, :], o_rows[c][:, t, P * j : P * j + P], ident[:])
            row = opool.tile([P, D], F32, name="out_row", bufs=6)
            copy(out=row[:].rearrange("c (m t) -> c m t", t=4), in_=bank[:].rearrange("c t m -> c m t"))
            nc.sync.dma_start(out=out_0[b0 + P * j : b0 + P * j + P, :], in_=row[:])

        tables = {"actx": {}, "mid": {}, "post": {}}

        def add(place, base, *call):
            tables[place[0]].setdefault(base + place[1], []).append(call)

        def emit(table, step):
            for call in tables[table].get(step, []):
                call[0](*call[1:])

        scopy, vcopy = nc.scalar.copy, nc.vector.tensor_copy
        copiers = {"s": scopy, "v": vcopy, "g": gcopy}
        scalers = {"s": scaled_copy_scalar, "v": scaled_copy_vector}
        groupers = {"g": planes_group_gpsimd, "v": planes_group_vector}
        n_chunks = len(CHUNKS)
        for c in range(n_chunks):
            b0, width = CHUNKS[c]
            last = last_unit[c]
            R = S["r"] if c < n_chunks - 2 else S["q"] if c == n_chunks - 2 else S["t"]
            for g in range(2 if c < n_chunks - 1 else 1):
                base = last - 2 + 2 * g
                add(R["ilg"][g], base, k_interleave, copiers[R["eng"][g][0]], c, g, 0, R["gs"][g])
                add(R["ila"][g], base, k_interleave, copiers[R["eng"][g][1]], c, g, R["gs"][g], R["hs"][g])
                add(R["ilb"][g], base, k_interleave, copiers[R["eng"][g][2]], c, g, R["hs"][g], 16)
                add(R["kq"][g], base, k_quantize, c, g)
            if c < n_chunks - 1:
                for t in range(4):
                    add(R["st"][t], last, stage2, c, t, scalers[R["oce"][t]], ps_t, "tr")
            if c < n_chunks - 2:
                add(R["pg"], last, groupers[R["pge"]], c)
                for j in range(width // P):
                    add(R["ot"][j], last, out_tile, c, j, copiers[R["ote"][j]])
                add(R["pq"], last, planes_quantize, c)
            if c > 1:
                first = 4 * c
                for j in range(width // P):
                    add(S["lf%d" % j], first, label_factor, c, j)
                for h in range(max(1, width // 256)):
                    add(S["xt%d" % h], first, x_transpose, c, h)
                    add(S["xm%d" % h], first, x_multiply, c, h)
                add(S["xq"], first, x_quantize, c)
        for h in range(2):
            add(S["hxt%d" % h], 0, x_transpose, 1, h)
            add(S["hxm%d" % h], 0, x_multiply, 1, h)
        for j in range(4):
            add(S["hlf%d" % j], 0, label_factor, 1, j)
        add(S["hxq"], 0, x_quantize, 1)
        for q in range(4):
            add(S["wt%d" % q], 0, w2_transpose, q // 2, q % 2, scopy)
        add(S["wq0"], 0, w2_quantize, 0)
        add(S["wq1"], 0, w2_quantize, 1)

        x_transpose(0, 0)
        x_multiply(0, 0)
        x_quantize(0)
        w1_interleave(scopy, 0, 1)
        w1_interleave(vcopy, 0, 0)
        constants()
        w1_quantize(0, 0)
        label_factor(0, 0)
        label_factor(0, 1)
        front(0)
        label_transpose(0)
        w1_quantize(0, 1)
        front(1)
        label_transpose(1)
        w1_interleave(scopy, 1, 1)
        w1_interleave(copiers[S["we"]], 1, 0)
        v1(0)
        emit("mid", -1)
        emit("actx", -1)
        emit("post", -1)
        w1_quantize(1, 0)
        w1_quantize(1, 1)
        n_units = len(units)
        for i in range(n_units):
            if i + 2 < n_units:
                front(i + 2)
            emit("actx", i)
            if i + 2 < n_units:
                label_transpose(i + 2)
            if i + 1 < n_units:
                v1(i + 1)
            emit("mid", i)
            if i < n_units:
                v2(i)
            emit("post", i)

        c = n_chunks - 1
        k_interleave(scopy, c, 1, 0, S["tl"])
        k_interleave(vcopy, c, 1, S["tl"], 16)
        k_quantize(c, 1)
        planes_group_gpsimd(c - 1)
        out_tile(c - 1, 0, scopy)
        out_tile(c - 1, 1, vcopy)
        out_tile(c - 1, 2, scopy)
        for t in range(4):
            stage2(c, t, scaled_copy_scalar if t % 2 == 0 else scaled_copy_vector, ps_s, "sb")
        out_tile(c - 1, 3, vcopy)
        planes_quantize(c - 1)
        scales_store(0, CHUNKS[c][0])
        out_tile(c, 0, scopy)
        out_tile(c, 1, vcopy)
        planes_group_vector(c)
        planes_quantize(c)
        scales_store(CHUNKS[c][0], B)
